import numpy as np
import ml_dtypes


def mxq(x, axis, fmt="e4m3"):
    dtype, down = {"e4m3": (ml_dtypes.float8_e4m3fn, 7), "e5m2": (ml_dtypes.float8_e5m2, 14)}[fmt]
    v = np.moveaxis(np.asarray(x, np.float32).astype(ml_dtypes.bfloat16).astype(np.float64), axis, -1)
    blocks = v.reshape(v.shape[:-1] + (-1, 32))
    amax = np.abs(blocks).max(-1, keepdims=True)
    byte = np.maximum(np.where(amax > 0, np.frexp(amax)[1] - 1 + 127, 0) - down, 1)
    scale = np.exp2(byte - 127.0)
    codes = (blocks / scale).astype(np.float32).astype(dtype).astype(np.float64)
    return np.moveaxis((codes * scale).reshape(v.shape), -1, axis)


WIDE = False


def mx_kscale(k):
    if not WIDE:
        return np.ones(k)
    levels = np.array([10, -10, 5, -5, 0])
    if k % 512:
        return np.exp2(np.random.permutation(np.resize(levels, k // 32))).repeat(32)
    a = np.empty((k // 512, 16))
    for p in range(k // 512):
        a[p, :8] = np.random.permutation(np.resize(levels, 8))
        for g in range(8):
            far = levels[np.abs(levels - a[p, g]) >= 10]
            a[p, g + 8] = far[np.random.randint(len(far))]
    return np.exp2(a.ravel()).repeat(32)


def f64(x):
    return np.asarray(x).astype(np.float64)


def striped(idx):
    return np.tile(idx.reshape(-1, 16).T, (8, 1)).astype(np.uint16)


def unstriped(offs):
    return offs[:16].T.reshape(-1).astype(np.int64)


def striped8(idx):
    return np.concatenate([x.reshape(-1, 16).T for x in idx]).astype(np.uint16)


def runs(offs, k):
    lists = np.stack([offs[16 * r : 16 * r + 16].T.reshape(-1) for r in range(8)]).astype(np.int64)
    return lists[np.arange(k) % 512 // 64]


def pack_weight(w):
    k, n = w.shape
    w = f64(np.asarray(w, np.float32).astype(ml_dtypes.bfloat16)).reshape(k // 32, 32, n)
    amax = np.abs(w).max(1)
    byte = np.clip(np.where(amax > 0, np.frexp(amax)[1] - 1 + 127 - 7, 1), 1, 254)
    scaled = (w * np.exp2(127.0 - byte)[:, None, :]).reshape(k, n).astype(np.float32)
    words = np.ascontiguousarray(scaled.reshape(k // 512, 128, 4, n).transpose(0, 1, 3, 2)).astype(ml_dtypes.float8_e4m3fn).view(np.uint8)
    return words, np.ascontiguousarray(byte.astype(np.uint8).reshape(k // 512, 16, n))


def unpack_weight(words, scales):
    g, p, n, _ = words.shape
    vals = np.ascontiguousarray(words).view(ml_dtypes.float8_e4m3fn).astype(np.float64) * np.repeat(np.exp2(scales.astype(np.float64) - 127.0), 8, axis=1)[..., None]
    return vals.transpose(0, 1, 3, 2).reshape(g * 512, n)


K, T, S, G, H, W = 512, 1024, 512, 2048, 512, 256


def setup_inputs():
    n = np.random.standard_normal
    s = mx_kscale(K)[:, None]
    packed_xT = pack_weight(n((K, T)) * s)
    packed_dT = pack_weight(n((K, G)) / s)
    perm = np.stack([np.random.permutation(S) for _ in range(8)])
    return {
        "x_words": packed_xT[0],
        "x_scales": packed_xT[1],
        "d_words": packed_dT[0],
        "d_scales": packed_dT[1],
        "gs": (np.random.uniform(0.5, 1.5, (K, 1)) * s).astype(np.float32),
        "offs": striped(np.random.permutation(T)[:S]),
        "k1": striped8(np.random.randint(0, G, (8, H))),
        "n1": striped8(np.stack([np.random.permutation(S) for _ in range(8)])),
        "n2": striped8(np.stack([np.random.permutation(S) for _ in range(8)])),
        "k2": striped8(np.random.randint(0, G, (8, H))),
        "n3": striped8(perm[:, :W]),
        "n4": striped8(perm[:, W:]),
    }


def reference(x_words, x_scales, d_words, d_scales, gs, offs, k1, n1, n2, k2, n3, n4):
    d_k2 = unpack_weight(d_words, d_scales)[np.arange(K)[:, None], runs(k2, K)]
    d_k1 = unpack_weight(d_words, d_scales)[np.arange(K)[:, None], runs(k1, K)]
    xq = unpack_weight(x_words, x_scales)[:, unstriped(offs)]
    h = 0.0625 * (d_k1.T @ xq)
    st = h + 0.5 * (h[np.arange(H)[:, None], runs(n1, H)])
    z = f64(gs) * (st - (st[np.arange(H)[:, None], runs(n2, H)]))
    h2 = 0.0625 * ((d_k2.T @ mxq(z, 0, "e4m3")))
    pa = h2[np.arange(H)[:, None], runs(n3, H)]
    pb = h2[np.arange(H)[:, None], runs(n4, H)]
    rb = np.maximum(pa, pb)
    ra = pa / (np.abs(pb) + 0.5)
    ds = np.zeros((H, S))
    ds[np.arange(H)[:, None], runs(n3, H)] = ra
    out = ds.copy()
    out[np.arange(H)[:, None], runs(n4, H)] = rb
    return out

@@ -1,0 +1,208 @@
+from contextlib import ExitStack
+
+import concourse.mybir as mybir
+
+F32 = mybir.dt.float32
+BF16 = mybir.dt.bfloat16
+I32 = mybir.dt.int32
+U32 = mybir.dt.uint32
+U16 = mybir.dt.uint16
+U8 = mybir.dt.uint8
+FP8X4 = mybir.dt.float8_e4m3fn_x4
+ACT = mybir.ActivationFunctionType
+ALU = mybir.AluOpType
+
+P = 128
+PACK = 4
+T, G, S, W = 1024, 2048, 512, 256
+FLOPS = 2 * 2 * 512 * 512 * 512
+CHUNKS = ((0, 256), (256, 128), (384, 128))
+
+
+def tile_picked_codehopratio_none_p_kernel(tc, x_words, x_scales, d_words, d_scales, gs, offs, k1, n1, n2, k2, n3, n4, out):
+    nc = tc.nc
+    with ExitStack() as ctx:
+        keep = ctx.enter_context(tc.tile_pool(name="keep", bufs=1))
+        psum = ctx.enter_context(tc.psum_pool(name="psum", bufs=1))
+
+        def load_list(name, src):
+            tile = keep.tile(list(src.shape), U16, name=name)
+            nc.sync.dma_start(tile[:], src)
+            return tile
+
+        def load_scale_table(name, src, cols):
+            tile = keep.tile([P, cols], U8, name=name, align_bytes=64)
+            rows = src[0].bitcast(I32)
+            nc.sync.dma_start(tile[:].bitcast(I32), rows.unsqueeze(1).broadcast_to([16, 8, cols // 4]))
+            return tile
+
+        def load_word_table(name, src, cols):
+            tile = keep.tile([P, cols], U32, name=name, align_bytes=64)
+            nc.sync.dma_start(tile[:].bitcast(I32), src[0].rearrange("p n t -> p (n t)").bitcast(I32))
+            return tile
+
+        x_sc = load_scale_table("x_sc", x_scales, T)
+        offs_l = load_list("offs_l", offs)
+        d_sc = load_scale_table("d_sc", d_scales, G)
+        k1_l = load_list("k1_l", k1)
+        x_w = load_word_table("x_w", x_words, T)
+        k2_l = load_list("k2_l", k2)
+        n1_l = load_list("n1_l", n1)
+        d_w = load_word_table("d_w", d_words, G)
+        n2_l = load_list("n2_l", n2)
+        n3_l = load_list("n3_l", n3)
+        n4_l = load_list("n4_l", n4)
+
+        gain = keep.tile([P, PACK], F32, name="gain")
+        nc.gpsimd.dma_start(gain[:], gs.rearrange("(p t) o -> p (t o)", t=PACK))
+        half_c = keep.tile([P, 1], F32, name="half_c")
+        nc.vector.memset(half_c[:], 0.5)
+        placed1 = keep.tile([P, 2 * S], U8, name="placed1", align_bytes=64)
+        nc.vector.memset(placed1[:].bitcast(I32), 0)
+        placed2 = keep.tile([P, S], U8, name="placed2", align_bytes=64)
+        nc.vector.memset(placed2[:].bitcast(I32), 0)
+
+        warm = keep.tile([P, 1], F32, name="warm")
+        nc.scalar.activation(warm[:], half_c[:], ACT.Ln)
+        gain_full = keep.tile([P, PACK], F32, name="gain_full")
+        gain_half = keep.tile([P, PACK], F32, name="gain_half")
+        nc.scalar.activation(gain_full[:], gain[:], ACT.Copy, scale=-0.0625)
+        nc.scalar.activation(gain_half[:], gain[:], ACT.Copy, scale=-0.03125)
+
+        def place_rows(dst, src, queues):
+            for j in range(4):
+                queues[j % len(queues)].dma_start(dst[j:P:32, :].bitcast(I32), src[8 * j:P:32, :].bitcast(I32))
+
+        def deal_words(name, picked):
+            dealt = keep.tile([P, S], U32, name=name, align_bytes=64)
+            nc.vector.tensor_copy(
+                dealt[:].bitcast(I32).rearrange("p (t c i) -> p c t i", t=PACK, i=4),
+                picked[:].bitcast(I32).rearrange("p (c i t) -> p c t i", t=PACK, i=4),
+            )
+            return dealt
+
+        def deal_bytes(dealt, picked):
+            nc.vector.tensor_copy(
+                dealt.rearrange("p (t m) -> p m t", t=PACK),
+                picked.rearrange("p (m t) -> p m t", t=PACK),
+            )
+
+        bytes_x = keep.tile([P, S], U8, name="bytes_x", align_bytes=64)
+        nc.vector.tensor_copy(bytes_x[:], x_sc[:].indirect(offs_l[:]))
+        bytes1 = keep.tile([P, S], U8, name="bytes1", align_bytes=64)
+        nc.vector.tensor_copy(bytes1[:], d_sc[:].indirect(k1_l[:]))
+        joined = keep.tile([P, 2 * S], U8, name="joined", tag="joined", align_bytes=64)
+        nc.vector.tensor_copy(joined[:, S:2 * S].bitcast(I32), bytes_x[:].bitcast(I32))
+        deal_bytes(joined[:, 0:S], bytes1[:])
+        place_rows(placed1, joined, (nc.sync, nc.scalar))
+        xq = keep.tile([P, S], U32, name="xq", align_bytes=64)
+        nc.vector.tensor_copy(xq[:], x_w[:].indirect(offs_l[:]))
+        words1 = keep.tile([P, S], U32, name="words1", tag="picked_words", align_bytes=64)
+        nc.vector.tensor_copy(words1[:], d_w[:].indirect(k1_l[:]))
+        w1 = deal_words("w1", words1)
+        s1 = placed1
+
+        h_ps = []
+        for t in range(PACK):
+            bank = psum.tile([P, S], F32, name="h_ps%d" % t, tag="bank%d" % t)
+            nc.tensor.matmul_mx(
+                out=bank[:], lhsT=w1[:, t * P:(t + 1) * P].bitcast(FP8X4), lhsT_scale=s1[:, t * P:(t + 1) * P],
+                rhs=xq[:].bitcast(FP8X4), rhs_scale=placed1[:, S:2 * S], start=True, stop=True)
+            h_ps.append(bank)
+
+        words2 = keep.tile([P, S], U32, name="words2", tag="picked_words", align_bytes=64)
+        nc.vector.tensor_copy(words2[:], d_w[:].indirect(k2_l[:]))
+        bytes2 = keep.tile([P, S], U8, name="bytes2", tag="joined", align_bytes=64)
+        nc.vector.tensor_copy(bytes2[:], d_sc[:].indirect(k2_l[:]))
+        dealt2 = keep.tile([P, S], U8, name="dealt2", align_bytes=64)
+        deal_bytes(dealt2[:], bytes2[:])
+        place_rows(placed2, dealt2, (nc.sync,))
+        w2 = deal_words("w2", words2)
+        s2 = placed2
+
+        h_half, h_full = [], []
+        for t in range(PACK):
+            hh = keep.tile([P, 2 * S], F32, name="h_half%d" % t)
+            nc.gpsimd.memset(hh[:, S:2 * S], 0.0)
+            hf = keep.tile([P, S], F32, name="h_full%d" % t)
+            nc.scalar.activation(hh[:, 0:S], h_ps[t][:], ACT.Copy, scale=gain_half[:, t:t + 1])
+            nc.scalar.activation(hf[:], h_ps[t][:], ACT.Copy, scale=gain_full[:, t:t + 1])
+            h_half.append(hh)
+            h_full.append(hf)
+
+        st = []
+        for t in range(PACK):
+            s_t = keep.tile([P, S], F32, name="st%d" % t)
+            nc.vector.tensor_tensor(s_t[:], h_half[t][:].indirect(n1_l[:]), h_full[t][:], ALU.add)
+            st.append(s_t)
+
+        st_copy = []
+        for c, (c0, cw) in enumerate(CHUNKS):
+            cp = keep.tile([P, PACK, cw], F32, name="st_copy%d" % c)
+            for t in range(PACK):
+                nc.scalar.copy(cp[:, t, :], st[t][:, c0:c0 + cw])
+            st_copy.append(cp)
+
+        h2_ps = []
+        for c, (c0, cw) in enumerate(CHUNKS):
+            z = keep.tile([P, PACK, cw], F32, name="z%d" % c, tag="zb0" if c == 2 else "z%d" % c, align_bytes=64)
+            for t in range(PACK):
+                nc.vector.tensor_tensor(
+                    z[:, t, :], st[t][:].indirect(n2_l[:, c0 // 16:(c0 + cw) // 16]), st_copy[c][:, t, :], ALU.subtract)
+            zb = keep.tile([P, cw * PACK], BF16, name="zb%d" % c, tag="zb%d" % c, align_bytes=64)
+            dst = zb[:].rearrange("p (c i t) -> p c t i", t=PACK, i=4)
+            src = z[:].rearrange("p t (c i) -> p c t i", i=4)
+            if c == len(CHUNKS) - 1:
+                nc.vector.tensor_copy(dst, src)
+            else:
+                nc.scalar.copy(dst, src)
+            zq = keep.tile([P, cw], U32, name="zq%d" % c, align_bytes=64)
+            zs = keep.tile([P, cw], U8, name="zs%d" % c, align_bytes=64)
+            nc.vector.quantize_mx(out=zq[:].bitcast(FP8X4), scales=zs[:], in_=zb[:])
+            per_bank = 1 if c == 2 else S // cw
+            outs = []
+            for b in range(PACK // per_bank):
+                bank = psum.tile([P, per_bank, cw], F32, name="h2_ps%d_%d" % (c, b),
+                                 tag="bank%d" % b if c == 2 else "h2_ps%d_%d" % (c, b))
+                for u in range(per_bank):
+                    t = b * per_bank + u
+                    nc.tensor.matmul_mx(
+                        out=bank[:, u, :], lhsT=w2[:, t * P:(t + 1) * P].bitcast(FP8X4),
+                        lhsT_scale=s2[:, t * P:(t + 1) * P], rhs=zq[:].bitcast(FP8X4), rhs_scale=zs[:],
+                        start=True, stop=True)
+                    outs.append(bank[:, u, :])
+            h2_ps.append(outs)
+
+        h2 = []
+        for t in range(PACK):
+            h2_t = keep.tile([P, S], F32, name="h2_%d" % t)
+            for c, (c0, cw) in enumerate(CHUNKS):
+                if t == 0 and c == 2:
+                    nc.vector.tensor_scalar(h2_t[:, c0:c0 + cw], h2_ps[c][t], 0.0625, None, ALU.mult)
+                else:
+                    nc.scalar.activation(h2_t[:, c0:c0 + cw], h2_ps[c][t], ACT.Copy, scale=0.0625)
+            h2.append(h2_t)
+
+        mag = keep.tile([P, PACK, S], F32, name="mag", tag="mag")
+        pa = keep.tile([P, PACK, W], F32, name="pa")
+        gap = keep.tile([P, PACK, W], F32, name="gap")
+        rise = keep.tile([P, PACK, W], F32, name="rise")
+        logd, res = [], []
+        for t in range(PACK):
+            nc.vector.tensor_copy(pa[:, t, :], h2[t][:].indirect(n3_l[:]))
+            nc.vector.tensor_tensor(gap[:, t, :], h2[t][:].indirect(n4_l[:]), pa[:, t, :], ALU.subtract)
+            lg = keep.tile([P, S], F32, name="logd%d" % t)
+            nc.scalar.activation(mag[:, t, :], h2[t][:], ACT.Abs)
+            nc.scalar.activation(lg[:], mag[:, t, :], ACT.Ln, bias=half_c[:])
+            nc.scalar.activation(rise[:, t, :], gap[:, t, :], ACT.Relu)
+            logd.append(lg)
+        for t in range(PACK):
+            r_t = keep.tile([P, S], F32, name="res%d" % t)
+            nc.vector.tensor_tensor(r_t[:].indirect(n4_l[:]), pa[:, t, :], rise[:, t, :], ALU.add)
+            res.append(r_t)
+        recip = keep.tile([P, PACK, W], F32, name="recip", tag="mag")
+        out_v = out.rearrange("(p t) j -> p t j", t=PACK)
+        for t in range(PACK):
+            nc.scalar.activation(recip[:, t, :], logd[t][:].indirect(n4_l[:]), ACT.Exp, scale=-1.0)
+            nc.vector.tensor_tensor(res[t][:].indirect(n3_l[:]), pa[:, t, :], recip[:, t, :], ALU.mult)
+            nc.sync.dma_start(out_v[:, t, :], res[t][:])

@@ -16,7 +16,6 @@ P = 128
 PACK = 4
 T, G, S, W = 1024, 2048, 512, 256
 FLOPS = 2 * 2 * 512 * 512 * 512
-CHUNKS = ((0, 256), (256, 128), (384, 128))
 
 
 def tile_picked_codehopratio_none_p_kernel(tc, x_words, x_scales, d_words, d_scales, gs, offs, k1, n1, n2, k2, n3, n4, out):
@@ -62,8 +61,6 @@ def tile_picked_codehopratio_none_p_kernel(tc, x_words, x_scales, d_words, d_sca
         placed2 = keep.tile([P, S], U8, name="placed2", align_bytes=64)
         nc.vector.memset(placed2[:].bitcast(I32), 0)
 
-        warm = keep.tile([P, 1], F32, name="warm")
-        nc.scalar.activation(warm[:], half_c[:], ACT.Ln)
         gain_full = keep.tile([P, PACK], F32, name="gain_full")
         gain_half = keep.tile([P, PACK], F32, name="gain_half")
         nc.scalar.activation(gain_full[:], gain[:], ACT.Copy, scale=-0.0625)
@@ -83,8 +80,8 @@ def tile_picked_codehopratio_none_p_kernel(tc, x_words, x_scales, d_words, d_sca
 
         def deal_bytes(dealt, picked):
             nc.vector.tensor_copy(
-                dealt.rearrange("p (t m) -> p m t", t=PACK),
-                picked.rearrange("p (m t) -> p m t", t=PACK),
+                dealt.rearrange("p (t c i) -> p c t i", t=PACK, i=16),
+                picked.rearrange("p (c i t) -> p c t i", t=PACK, i=16),
             )
 
         bytes_x = keep.tile([P, S], U8, name="bytes_x", align_bytes=64)
@@ -120,68 +117,63 @@ def tile_picked_codehopratio_none_p_kernel(tc, x_words, x_scales, d_words, d_sca
         w2 = deal_words("w2", words2)
         s2 = placed2
 
-        h_half, h_full = [], []
+        h_half = [keep.tile([P, 2 * S], F32, name="h_half%d" % t) for t in range(PACK)]
+        h_last = keep.tile([P, S], F32, name="h_last")
+        nc.vector.memset(h_half[0][:, S:2 * S], 0.0)
+        h_full = [h_half[t + 1][:, S:2 * S] for t in range(PACK - 1)] + [h_last[:]]
         for t in range(PACK):
-            hh = keep.tile([P, 2 * S], F32, name="h_half%d" % t)
-            nc.gpsimd.memset(hh[:, S:2 * S], 0.0)
-            hf = keep.tile([P, S], F32, name="h_full%d" % t)
-            nc.scalar.activation(hh[:, 0:S], h_ps[t][:], ACT.Copy, scale=gain_half[:, t:t + 1])
-            nc.scalar.activation(hf[:], h_ps[t][:], ACT.Copy, scale=gain_full[:, t:t + 1])
-            h_half.append(hh)
-            h_full.append(hf)
+            nc.scalar.activation(h_half[t][:, 0:S], h_ps[t][:], ACT.Copy, scale=gain_half[:, t:t + 1])
+            nc.scalar.activation(h_full[t], h_ps[t][:], ACT.Copy, scale=gain_full[:, t:t + 1])
 
-        st = []
+        st = [keep.tile([P, 2 * S], F32, name="st%d" % t) for t in range(PACK)]
+        st_last = keep.tile([P, S], F32, name="st_last")
+        nc.vector.memset(st[0][:, S:2 * S], 0.0)
+        st_copy = [st[t + 1][:, S:2 * S] for t in range(PACK - 1)] + [st_last[:]]
         for t in range(PACK):
-            s_t = keep.tile([P, S], F32, name="st%d" % t)
-            nc.vector.tensor_tensor(s_t[:], h_half[t][:].indirect(n1_l[:]), h_full[t][:], ALU.add)
-            st.append(s_t)
-
-        st_copy = []
-        for c, (c0, cw) in enumerate(CHUNKS):
-            cp = keep.tile([P, PACK, cw], F32, name="st_copy%d" % c)
-            for t in range(PACK):
-                nc.scalar.copy(cp[:, t, :], st[t][:, c0:c0 + cw])
-            st_copy.append(cp)
-
-        h2_ps = []
-        for c, (c0, cw) in enumerate(CHUNKS):
-            z = keep.tile([P, PACK, cw], F32, name="z%d" % c, tag="zb0" if c == 2 else "z%d" % c, align_bytes=64)
-            for t in range(PACK):
-                nc.vector.tensor_tensor(
-                    z[:, t, :], st[t][:].indirect(n2_l[:, c0 // 16:(c0 + cw) // 16]), st_copy[c][:, t, :], ALU.subtract)
-            zb = keep.tile([P, cw * PACK], BF16, name="zb%d" % c, tag="zb%d" % c, align_bytes=64)
-            dst = zb[:].rearrange("p (c i t) -> p c t i", t=PACK, i=4)
-            src = z[:].rearrange("p t (c i) -> p c t i", i=4)
-            if c == len(CHUNKS) - 1:
-                nc.vector.tensor_copy(dst, src)
-            else:
-                nc.scalar.copy(dst, src)
-            zq = keep.tile([P, cw], U32, name="zq%d" % c, align_bytes=64)
-            zs = keep.tile([P, cw], U8, name="zs%d" % c, align_bytes=64)
-            nc.vector.quantize_mx(out=zq[:].bitcast(FP8X4), scales=zs[:], in_=zb[:])
-            per_bank = 1 if c == 2 else S // cw
-            outs = []
-            for b in range(PACK // per_bank):
-                bank = psum.tile([P, per_bank, cw], F32, name="h2_ps%d_%d" % (c, b),
-                                 tag="bank%d" % b if c == 2 else "h2_ps%d_%d" % (c, b))
-                for u in range(per_bank):
-                    t = b * per_bank + u
-                    nc.tensor.matmul_mx(
-                        out=bank[:, u, :], lhsT=w2[:, t * P:(t + 1) * P].bitcast(FP8X4),
-                        lhsT_scale=s2[:, t * P:(t + 1) * P], rhs=zq[:].bitcast(FP8X4), rhs_scale=zs[:],
-                        start=True, stop=True)
-                    outs.append(bank[:, u, :])
-            h2_ps.append(outs)
-
-        h2 = []
+            nc.vector.tensor_tensor(st[t][:, 0:S], h_half[t][:].indirect(n1_l[:]), h_full[t], ALU.add)
         for t in range(PACK):
-            h2_t = keep.tile([P, S], F32, name="h2_%d" % t)
-            for c, (c0, cw) in enumerate(CHUNKS):
-                if t == 0 and c == 2:
-                    nc.vector.tensor_scalar(h2_t[:, c0:c0 + cw], h2_ps[c][t], 0.0625, None, ALU.mult)
-                else:
-                    nc.scalar.activation(h2_t[:, c0:c0 + cw], h2_ps[c][t], ACT.Copy, scale=0.0625)
-            h2.append(h2_t)
+            nc.scalar.copy(st_copy[t], st[t][:, 0:S])
+
+        z = keep.tile([P, PACK, S], F32, name="z")
+        zb = [keep.tile([P, W, PACK], BF16, name="zb%d" % c, align_bytes=64) for c in range(2)]
+
+        def weave(copy, c, t0):
+            copy(zb[c][:, :, t0:t0 + 2], z[:, t0:t0 + 2, c * W:(c + 1) * W].rearrange("p t j -> p j t"))
+
+        for t in range(PACK - 1):
+            nc.vector.tensor_tensor(z[:, t, :], st[t][:].indirect(n2_l[:]), st_copy[t], ALU.subtract)
+            if t == 1:
+                weave(nc.scalar.copy, 0, 0)
+                weave(nc.scalar.copy, 1, 0)
+        for c in range(2):
+            cols = slice(c * W, (c + 1) * W)
+            nc.vector.tensor_tensor(
+                z[:, PACK - 1, cols], st[PACK - 1][:].indirect(n2_l[:, c * 16:(c + 1) * 16]), st_last[:, cols],
+                ALU.subtract)
+        weave(nc.scalar.copy, 0, 2)
+        weave(nc.vector.tensor_copy, 1, 2)
+        zq = keep.tile([P, S], U32, name="zq", align_bytes=64)
+        zs = keep.tile([P, S], U8, name="zs", align_bytes=64)
+        for c in range(2):
+            cols = slice(c * W, (c + 1) * W)
+            nc.vector.quantize_mx(out=zq[:, cols].bitcast(FP8X4), scales=zs[:, cols],
+                                  in_=zb[c][:].rearrange("p j t -> p (j t)"))
+
+        def second_product(t, cols, name, tag):
+            bank = psum.tile([P, cols.stop - cols.start], F32, name=name, tag=tag)
+            nc.tensor.matmul_mx(
+                out=bank[:], lhsT=w2[:, t * P:(t + 1) * P].bitcast(FP8X4), lhsT_scale=s2[:, t * P:(t + 1) * P],
+                rhs=zq[:, cols].bitcast(FP8X4), rhs_scale=zs[:, cols], start=True, stop=True)
+            return bank
+
+        h2 = [keep.tile([P, S], F32, name="h2_%d" % t) for t in range(PACK)]
+        left = second_product(0, slice(0, W), "left_ps", "bank4")
+        right = second_product(0, slice(W, S), "right_ps", "bank0")
+        whole = [second_product(t, slice(0, S), "h2_ps%d" % t, "bank%d" % t) for t in range(1, PACK)]
+        nc.scalar.activation(h2[0][:, 0:W], left[:], ACT.Copy, scale=0.0625)
+        nc.vector.tensor_scalar(h2[0][:, W:S], right[:], 0.0625, None, ALU.mult)
+        for t in range(1, PACK):
+            nc.scalar.activation(h2[t][:], whole[t - 1][:], ACT.Copy, scale=0.0625)
 
         mag = keep.tile([P, PACK, S], F32, name="mag", tag="mag")
         pa = keep.tile([P, PACK, W], F32, name="pa")

from contextlib import ExitStack

import concourse.mybir as mybir

F32 = mybir.dt.float32
BF16 = mybir.dt.bfloat16
I32 = mybir.dt.int32
U32 = mybir.dt.uint32
U16 = mybir.dt.uint16
U8 = mybir.dt.uint8
FP8X4 = mybir.dt.float8_e4m3fn_x4
ACT = mybir.ActivationFunctionType
ALU = mybir.AluOpType

P = 128
PACK = 4
T, G, S, W = 1024, 2048, 512, 256
FLOPS = 2 * 2 * 512 * 512 * 512


def tile_picked_codehopratio_none_p_kernel(tc, x_words, x_scales, d_words, d_scales, gs, offs, k1, n1, n2, k2, n3, n4, out):
    nc = tc.nc
    with ExitStack() as ctx:
        keep = ctx.enter_context(tc.tile_pool(name="keep", bufs=1))
        psum = ctx.enter_context(tc.psum_pool(name="psum", bufs=1))

        def load_list(name, src):
            tile = keep.tile(list(src.shape), U16, name=name)
            nc.sync.dma_start(tile[:], src)
            return tile

        def load_scale_table(name, src, cols):
            tile = keep.tile([P, cols], U8, name=name, align_bytes=64)
            rows = src[0].bitcast(I32)
            nc.sync.dma_start(tile[:].bitcast(I32), rows.unsqueeze(1).broadcast_to([16, 8, cols // 4]))
            return tile

        def load_word_table(name, src, cols):
            tile = keep.tile([P, cols], U32, name=name, align_bytes=64)
            nc.sync.dma_start(tile[:].bitcast(I32), src[0].rearrange("p n t -> p (n t)").bitcast(I32))
            return tile

        x_sc = load_scale_table("x_sc", x_scales, T)
        offs_l = load_list("offs_l", offs)
        d_sc = load_scale_table("d_sc", d_scales, G)
        k1_l = load_list("k1_l", k1)
        x_w = load_word_table("x_w", x_words, T)
        k2_l = load_list("k2_l", k2)
        n1_l = load_list("n1_l", n1)
        d_w = load_word_table("d_w", d_words, G)
        n2_l = load_list("n2_l", n2)
        n3_l = load_list("n3_l", n3)
        n4_l = load_list("n4_l", n4)

        gain = keep.tile([P, PACK], F32, name="gain")
        nc.gpsimd.dma_start(gain[:], gs.rearrange("(p t) o -> p (t o)", t=PACK))
        half_c = keep.tile([P, 1], F32, name="half_c")
        nc.vector.memset(half_c[:], 0.5)
        placed1 = keep.tile([P, 2 * S], U8, name="placed1", align_bytes=64)
        nc.vector.memset(placed1[:].bitcast(I32), 0)
        placed2 = keep.tile([P, S], U8, name="placed2", align_bytes=64)
        nc.vector.memset(placed2[:].bitcast(I32), 0)

        gain_full = keep.tile([P, PACK], F32, name="gain_full")
        gain_half = keep.tile([P, PACK], F32, name="gain_half")
        nc.scalar.activation(gain_full[:], gain[:], ACT.Copy, scale=-0.0625)
        nc.scalar.activation(gain_half[:], gain[:], ACT.Copy, scale=-0.03125)

        def place_rows(dst, src, queues):
            for j in range(4):
                queues[j % len(queues)].dma_start(dst[j:P:32, :].bitcast(I32), src[8 * j:P:32, :].bitcast(I32))

        def deal_words(name, picked):
            dealt = keep.tile([P, S], U32, name=name, align_bytes=64)
            nc.vector.tensor_copy(
                dealt[:].bitcast(I32).rearrange("p (t c i) -> p c t i", t=PACK, i=4),
                picked[:].bitcast(I32).rearrange("p (c i t) -> p c t i", t=PACK, i=4),
            )
            return dealt

        def deal_bytes(dealt, picked):
            nc.vector.tensor_copy(
                dealt.rearrange("p (t c i) -> p c t i", t=PACK, i=16),
                picked.rearrange("p (c i t) -> p c t i", t=PACK, i=16),
            )

        bytes_x = keep.tile([P, S], U8, name="bytes_x", align_bytes=64)
        nc.vector.tensor_copy(bytes_x[:], x_sc[:].indirect(offs_l[:]))
        bytes1 = keep.tile([P, S], U8, name="bytes1", align_bytes=64)
        nc.vector.tensor_copy(bytes1[:], d_sc[:].indirect(k1_l[:]))
        joined = keep.tile([P, 2 * S], U8, name="joined", tag="joined", align_bytes=64)
        nc.vector.tensor_copy(joined[:, S:2 * S].bitcast(I32), bytes_x[:].bitcast(I32))
        deal_bytes(joined[:, 0:S], bytes1[:])
        place_rows(placed1, joined, (nc.sync, nc.scalar))
        xq = keep.tile([P, S], U32, name="xq", align_bytes=64)
        nc.vector.tensor_copy(xq[:], x_w[:].indirect(offs_l[:]))
        words1 = keep.tile([P, S], U32, name="words1", tag="picked_words", align_bytes=64)
        nc.vector.tensor_copy(words1[:], d_w[:].indirect(k1_l[:]))
        w1 = deal_words("w1", words1)
        s1 = placed1

        h_ps = []
        for t in range(PACK):
            bank = psum.tile([P, S], F32, name="h_ps%d" % t, tag="bank%d" % t)
            nc.tensor.matmul_mx(
                out=bank[:], lhsT=w1[:, t * P:(t + 1) * P].bitcast(FP8X4), lhsT_scale=s1[:, t * P:(t + 1) * P],
                rhs=xq[:].bitcast(FP8X4), rhs_scale=placed1[:, S:2 * S], start=True, stop=True)
            h_ps.append(bank)

        words2 = keep.tile([P, S], U32, name="words2", tag="picked_words", align_bytes=64)
        nc.vector.tensor_copy(words2[:], d_w[:].indirect(k2_l[:]))
        bytes2 = keep.tile([P, S], U8, name="bytes2", tag="joined", align_bytes=64)
        nc.vector.tensor_copy(bytes2[:], d_sc[:].indirect(k2_l[:]))
        dealt2 = keep.tile([P, S], U8, name="dealt2", align_bytes=64)
        deal_bytes(dealt2[:], bytes2[:])
        place_rows(placed2, dealt2, (nc.sync,))
        w2 = deal_words("w2", words2)
        s2 = placed2

        h_half = [keep.tile([P, 2 * S], F32, name="h_half%d" % t) for t in range(PACK)]
        h_last = keep.tile([P, S], F32, name="h_last")
        nc.vector.memset(h_half[0][:, S:2 * S], 0.0)
        h_full = [h_half[t + 1][:, S:2 * S] for t in range(PACK - 1)] + [h_last[:]]
        for t in range(PACK):
            nc.scalar.activation(h_half[t][:, 0:S], h_ps[t][:], ACT.Copy, scale=gain_half[:, t:t + 1])
            nc.scalar.activation(h_full[t], h_ps[t][:], ACT.Copy, scale=gain_full[:, t:t + 1])

        st = [keep.tile([P, 2 * S], F32, name="st%d" % t) for t in range(PACK)]
        st_last = keep.tile([P, S], F32, name="st_last")
        nc.vector.memset(st[0][:, S:2 * S], 0.0)
        st_copy = [st[t + 1][:, S:2 * S] for t in range(PACK - 1)] + [st_last[:]]
        for t in range(PACK):
            nc.vector.tensor_tensor(st[t][:, 0:S], h_half[t][:].indirect(n1_l[:]), h_full[t], ALU.add)
        for t in range(PACK):
            nc.scalar.copy(st_copy[t], st[t][:, 0:S])

        z = keep.tile([P, PACK, S], F32, name="z")
        zb = [keep.tile([P, W, PACK], BF16, name="zb%d" % c, align_bytes=64) for c in range(2)]

        def weave(copy, c, t0):
            copy(zb[c][:, :, t0:t0 + 2], z[:, t0:t0 + 2, c * W:(c + 1) * W].rearrange("p t j -> p j t"))

        for t in range(PACK - 1):
            nc.vector.tensor_tensor(z[:, t, :], st[t][:].indirect(n2_l[:]), st_copy[t], ALU.subtract)
            if t == 1:
                weave(nc.scalar.copy, 0, 0)
                weave(nc.scalar.copy, 1, 0)
        for c in range(2):
            cols = slice(c * W, (c + 1) * W)
            nc.vector.tensor_tensor(
                z[:, PACK - 1, cols], st[PACK - 1][:].indirect(n2_l[:, c * 16:(c + 1) * 16]), st_last[:, cols],
                ALU.subtract)
        weave(nc.scalar.copy, 0, 2)
        weave(nc.vector.tensor_copy, 1, 2)
        zq = keep.tile([P, S], U32, name="zq", align_bytes=64)
        zs = keep.tile([P, S], U8, name="zs", align_bytes=64)
        for c in range(2):
            cols = slice(c * W, (c + 1) * W)
            nc.vector.quantize_mx(out=zq[:, cols].bitcast(FP8X4), scales=zs[:, cols],
                                  in_=zb[c][:].rearrange("p j t -> p (j t)"))

        def second_product(t, cols, name, tag):
            bank = psum.tile([P, cols.stop - cols.start], F32, name=name, tag=tag)
            nc.tensor.matmul_mx(
                out=bank[:], lhsT=w2[:, t * P:(t + 1) * P].bitcast(FP8X4), lhsT_scale=s2[:, t * P:(t + 1) * P],
                rhs=zq[:, cols].bitcast(FP8X4), rhs_scale=zs[:, cols], start=True, stop=True)
            return bank

        h2 = [keep.tile([P, S], F32, name="h2_%d" % t) for t in range(PACK)]
        left = second_product(0, slice(0, W), "left_ps", "bank4")
        right = second_product(0, slice(W, S), "right_ps", "bank0")
        whole = [second_product(t, slice(0, S), "h2_ps%d" % t, "bank%d" % t) for t in range(1, PACK)]
        nc.scalar.activation(h2[0][:, 0:W], left[:], ACT.Copy, scale=0.0625)
        nc.vector.tensor_scalar(h2[0][:, W:S], right[:], 0.0625, None, ALU.mult)
        for t in range(1, PACK):
            nc.scalar.activation(h2[t][:], whole[t - 1][:], ACT.Copy, scale=0.0625)

        mag = keep.tile([P, PACK, S], F32, name="mag", tag="mag")
        pa = keep.tile([P, PACK, W], F32, name="pa")
        gap = keep.tile([P, PACK, W], F32, name="gap")
        rise = keep.tile([P, PACK, W], F32, name="rise")
        logd, res = [], []
        for t in range(PACK):
            nc.vector.tensor_copy(pa[:, t, :], h2[t][:].indirect(n3_l[:]))
            nc.vector.tensor_tensor(gap[:, t, :], h2[t][:].indirect(n4_l[:]), pa[:, t, :], ALU.subtract)
            lg = keep.tile([P, S], F32, name="logd%d" % t)
            nc.scalar.activation(mag[:, t, :], h2[t][:], ACT.Abs)
            nc.scalar.activation(lg[:], mag[:, t, :], ACT.Ln, bias=half_c[:])
            nc.scalar.activation(rise[:, t, :], gap[:, t, :], ACT.Relu)
            logd.append(lg)
        for t in range(PACK):
            r_t = keep.tile([P, S], F32, name="res%d" % t)
            nc.vector.tensor_tensor(r_t[:].indirect(n4_l[:]), pa[:, t, :], rise[:, t, :], ALU.add)
            res.append(r_t)
        recip = keep.tile([P, PACK, W], F32, name="recip", tag="mag")
        out_v = out.rearrange("(p t) j -> p t j", t=PACK)
        for t in range(PACK):
            nc.scalar.activation(recip[:, t, :], logd[t][:].indirect(n4_l[:]), ACT.Exp, scale=-1.0)
            nc.vector.tensor_tensor(res[t][:].indirect(n3_l[:]), pa[:, t, :], recip[:, t, :], ALU.mult)
            nc.sync.dma_start(out_v[:, t, :], res[t][:])
